import numpy as np
import ml_dtypes


def mxq(x, axis, fmt="e4m3"):
    dtype, down = {"e4m3": (ml_dtypes.float8_e4m3fn, 7), "e5m2": (ml_dtypes.float8_e5m2, 14)}[fmt]
    v = np.moveaxis(np.asarray(x, np.float32).astype(ml_dtypes.bfloat16).astype(np.float64), axis, -1)
    blocks = v.reshape(v.shape[:-1] + (-1, 32))
    amax = np.abs(blocks).max(-1, keepdims=True)
    byte = np.maximum(np.where(amax > 0, np.frexp(amax)[1] - 1 + 127, 0) - down, 1)
    scale = np.exp2(byte - 127.0)
    codes = (blocks / scale).astype(np.float32).astype(dtype).astype(np.float64)
    return np.moveaxis((codes * scale).reshape(v.shape), -1, axis)


WIDE = False


def mx_kscale(k):
    if not WIDE:
        return np.ones(k)
    levels = np.array([10, -10, 5, -5, 0])
    if k % 512:
        return np.exp2(np.random.permutation(np.resize(levels, k // 32))).repeat(32)
    a = np.empty((k // 512, 16))
    for p in range(k // 512):
        a[p, :8] = np.random.permutation(np.resize(levels, 8))
        for g in range(8):
            far = levels[np.abs(levels - a[p, g]) >= 10]
            a[p, g + 8] = far[np.random.randint(len(far))]
    return np.exp2(a.ravel()).repeat(32)


BF16 = ml_dtypes.bfloat16


def bf(x):
    return np.asarray(x, np.float32).astype(BF16)


def f64(x):
    return np.asarray(x).astype(np.float64)

def planes(Y):
    n, m = Y.shape
    b = f64(bf(Y)).reshape(n // 32, 32, m)
    amax = np.abs(b).max(1)
    byte = np.clip(np.where(amax > 0, np.frexp(amax)[1] - 1 + 127 - 7, 1), 1, 254)
    codes = (b * np.exp2(127.0 - byte)[:, None, :]).reshape(n, m).astype(np.float32).astype(ml_dtypes.float8_e4m3fn).view(np.uint8)
    words = codes.reshape(n // 512, 128, 4, m).transpose(0, 1, 3, 2)
    return np.ascontiguousarray(words), np.ascontiguousarray(byte.astype(np.uint8).reshape(n // 512, 16, m))


S, B, D, R, F = 4, 384, 1024, 512, 1024


def setup_inputs():
    s, t = mx_kscale(R), mx_kscale(D)
    return {
        "x": bf(np.random.standard_normal((S, B, D)) / t),
        "mu": bf(np.random.standard_normal((D, F)) / np.sqrt(D) * t[:, None]),
        "u": bf(np.random.standard_normal((D, R)) / np.sqrt(R) * s[None, :] * t[:, None]),
        "noise": bf(np.random.standard_normal((S, R, F)) / s[:, None]),
        "colscale": bf(np.random.uniform(0.5, 1.5, F) / np.sqrt(D)),
        "b": bf(np.random.standard_normal(F) * 0.3),
    }


def sample_weights(mu, u, noise, colscale):
    a = mxq(u, 1, "e4m3") @ mxq(noise, 1, "e4m3")
    return mu[None, :, :] + a * colscale[None, None, :]


def core(x, mu, u, noise, colscale, b):
    w = sample_weights(f64(mu), f64(u), f64(noise), f64(colscale))
    y = mxq(f64(x), 2, "e4m3") @ mxq(w, 1, "e4m3")
    return y + f64(b)[None, None, :]


def reference(x, mu, u, noise, colscale, b):
    R_out = core(x, mu, u, noise, colscale, b)
    words, scales = planes(np.moveaxis(R_out, 2, 0).reshape(1024, -1))
    return R_out, words, scales

@@ -1,0 +1,335 @@
+from contextlib import ExitStack
+
+import concourse.mybir as mybir
+from concourse.masks import make_identity
+
+F32 = mybir.dt.float32
+BF16 = mybir.dt.bfloat16
+I32 = mybir.dt.int32
+U32 = mybir.dt.uint32
+U8 = mybir.dt.uint8
+FP8X4 = mybir.dt.float8_e4m3fn_x4
+MULT = mybir.AluOpType.mult
+ADD = mybir.AluOpType.add
+
+S, B, D, R, F = 4, 384, 1024, 512, 1024
+FLOPS = 2 * S * D * R * F + 2 * S * B * D * F
+P = 128
+
+
+def tile_matrixvariategaussiansampledweights_x1_kernel(tc, x, mu, u, noise, colscale, b, out_0, out_1, out_2):
+    nc = tc.nc
+    with ExitStack() as ctx:
+        const = ctx.enter_context(tc.tile_pool(name="const", bufs=1))
+        raw = ctx.enter_context(tc.tile_pool(name="raw", bufs=1))
+        work = ctx.enter_context(tc.tile_pool(name="work", bufs=3))
+        acc_pool = ctx.enter_context(tc.psum_pool(name="acc_pool", bufs=5))
+        tr_pool = ctx.enter_context(tc.psum_pool(name="tr_pool", bufs=3))
+
+        n_raw = {}
+        for s in range(S):
+            n_raw[s] = raw.tile([P, 4, F], BF16, name="n_raw%d" % s, align_bytes=64)
+        u_raw = {}
+        mu_raw = {}
+        for g in range(2):
+            u_raw[g] = raw.tile([P, 4, R], BF16, name="u_raw%d" % g, align_bytes=64)
+            for fh in range(2):
+                mu_raw[g, fh] = raw.tile([P, 4, 512], BF16, name="mu_raw%d%d" % (g, fh), align_bytes=64)
+        x_raw = {}
+        for s in range(S):
+            x_raw[s] = raw.tile([P, 3, D], BF16, name="x_raw%d" % s, align_bytes=64)
+        cs_rows = const.tile([P, P], BF16, name="cs_rows", align_bytes=64)
+        b_all = const.tile([P, F], BF16, name="b_all", align_bytes=64)
+        nc.vector.memset(cs_rows[:], 0.0)
+
+        def load_noise_half(s, fh):
+            cols = slice(512 * fh, 512 * fh + 512)
+            nc.sync.dma_start(out=n_raw[s][:, :, cols], in_=noise[s, :, cols].rearrange("(p j) f -> p j f", j=4))
+
+        def load_u(g):
+            nc.sync.dma_start(out=u_raw[g][:], in_=u[512 * g : 512 * g + 512, :].rearrange("(q j) r -> q j r", j=4))
+
+        def load_mu(g, fh):
+            cols = slice(512 * fh, 512 * fh + 512)
+            nc.sync.dma_start(out=mu_raw[g, fh][:], in_=mu[512 * g : 512 * g + 512, cols].rearrange("(q j) f -> q j f", j=4))
+
+        def load_x(s):
+            nc.sync.dma_start(out=x_raw[s][:], in_=x[s].rearrange("(m p) d -> p m d", p=P))
+
+        load_u(0)
+        load_noise_half(0, 0)
+        nc.sync.dma_start(out=cs_rows[0:8, :], in_=colscale.rearrange("(c p) -> c p", p=P))
+        load_mu(0, 0)
+        load_u(1)
+        load_mu(1, 0)
+        load_x(0)
+        load_noise_half(0, 1)
+        load_mu(0, 1)
+        load_mu(1, 1)
+        nc.sync.dma_start(out=b_all[:], in_=b.partition_broadcast(P))
+        for s in range(1, S):
+            nc.sync.dma_start(out=n_raw[s][:], in_=noise[s].rearrange("(p j) f -> p j f", j=4))
+            load_x(s)
+
+        ident_f32 = const.tile([P, P], F32, name="ident_f32", align_bytes=64)
+        make_identity(nc, ident_f32[:])
+        ident_bf16 = const.tile([P, P], BF16, name="ident_bf16", align_bytes=64)
+        make_identity(nc, ident_bf16[:])
+
+        cs = const.tile([P, 8], F32, name="cs")
+        mu_t = const.tile([P, 8, D], BF16, name="mu_t", align_bytes=64)
+        u_codes, u_scales = {}, {}
+        n_codes, n_scales = {}, {}
+        x_codes, x_scales = {}, {}
+        w_codes, w_scales = {}, {}
+        w_t, w_grp = {}, {}
+        n_grp, x_grp = {}, {}
+        o_f32, o_bf, o_grp = {}, {}, {}
+        o_codes, o_scales = {}, {}
+        copy_v = nc.vector.tensor_copy
+        copy_s = nc.scalar.copy
+
+        def prep_cs():
+            ps = tr_pool.tile([P, P], BF16, name="tr")
+            nc.tensor.transpose(ps[:], cs_rows[:], ident_bf16[:])
+            copy_v(out=cs[:], in_=ps[:, 0:8])
+
+        def prep_u(g, copies):
+            grp = work.tile([P, 2048], BF16, name="u_grp", align_bytes=64, bufs=2)
+            for u2 in range(2):
+                ps = tr_pool.tile([P, 512], F32, name="tr")
+                for e in range(2):
+                    words = u_raw[g][:, 2 * u2 + e, :].bitcast(F32)
+                    for h in range(2):
+                        c0 = 128 * (2 * e + h)
+                        nc.tensor.transpose(ps[:, c0 : c0 + 128], words[:, h : 256 : 2], ident_f32[:])
+                copies[u2](
+                    out=grp[:].bitcast(F32)[:, 512 * u2 : 512 * u2 + 512].rearrange("p (q e h) -> p q e h", e=2, h=2),
+                    in_=ps[:].rearrange("p (e h q) -> p q e h", e=2, h=2),
+                )
+            u_codes[g] = const.tile([P, 512], U32, name="u_codes%d" % g, align_bytes=64)
+            u_scales[g] = const.tile([P, 512], U8, name="u_scales%d" % g, align_bytes=64)
+            nc.vector.quantize_mx(out=u_codes[g][:].bitcast(FP8X4), scales=u_scales[g][:], in_=grp[:])
+
+        def prep_mu(g, ft, copy):
+            ps = tr_pool.tile([P, 512], BF16, name="tr")
+            c0 = 128 * (ft % 4)
+            for j in range(4):
+                nc.tensor.transpose(ps[:, 128 * j : 128 * j + 128], mu_raw[g, ft // 4][:, j, c0 : c0 + 128], ident_bf16[:])
+            copy(
+                out=mu_t[:, ft, 512 * g : 512 * g + 512].rearrange("p (v q e) -> p v q e", v=2, e=2),
+                in_=ps[:].rearrange("p (v e q) -> p v q e", v=2, e=2),
+            )
+
+        def noise_copy(s, fh, copy, part, parts):
+            if part == 0:
+                n_grp[s, fh] = work.tile([P, 512, 4], BF16, name="n_grp", align_bytes=64, bufs=3)
+            w = 512 // parts
+            lo = w * part
+            copy(
+                out=n_grp[s, fh][:, lo : lo + w, :],
+                in_=n_raw[s][:, :, 512 * fh + lo : 512 * fh + lo + w].rearrange("p j f -> p f j"),
+            )
+
+        def noise_quant(s, fh):
+            n_codes[s, fh] = work.tile([P, 512], U32, name="n_codes", align_bytes=64, bufs=4)
+            n_scales[s, fh] = work.tile([P, 512], U8, name="n_scales", align_bytes=64, bufs=4)
+            nc.vector.quantize_mx(
+                out=n_codes[s, fh][:].bitcast(FP8X4),
+                scales=n_scales[s, fh][:],
+                in_=n_grp[s, fh][:].rearrange("p f j -> p (f j)"),
+            )
+
+        def x_turn(s, m, copy):
+            ps = tr_pool.tile([P, 512], F32, name="tr")
+            words = x_raw[s][:, m, :].bitcast(F32)
+            for g in range(2):
+                for v in range(2):
+                    c0 = 128 * (2 * g + v)
+                    nc.tensor.transpose(ps[:, c0 : c0 + 128], words[:, 256 * g + v : 256 * g + 256 : 2], ident_f32[:])
+            x_grp[s, m] = work.tile([P, 1024], BF16, name="x_grp", align_bytes=64, bufs=4)
+            copy(
+                out=x_grp[s, m][:].bitcast(F32).rearrange("p (g r v) -> p g r v", g=2, v=2),
+                in_=ps[:].rearrange("p (g v r) -> p g r v", g=2, v=2),
+            )
+
+        def x_quant(s, m):
+            x_codes[s, m] = work.tile([P, 256], U32, name="x_codes", align_bytes=64, bufs=7)
+            x_scales[s, m] = work.tile([P, 256], U8, name="x_scales", align_bytes=64, bufs=7)
+            nc.vector.quantize_mx(out=x_codes[s, m][:].bitcast(FP8X4), scales=x_scales[s, m][:], in_=x_grp[s, m][:])
+
+        accs = {}
+
+        def stage1_mx(k):
+            s, fh, g = k // 4, (k // 2) % 2, k % 2
+            for t in range(4):
+                accs[k, t] = acc_pool.tile([P, 512], F32, name="acc")
+                cols = slice(128 * t, 128 * t + 128)
+                nc.tensor.matmul_mx(
+                    out=accs[k, t][:],
+                    lhsT=n_codes[s, fh][:, cols].bitcast(FP8X4),
+                    lhsT_scale=n_scales[s, fh][:, cols],
+                    rhs=u_codes[g][:].bitcast(FP8X4),
+                    rhs_scale=u_scales[g][:],
+                    start=True,
+                    stop=True,
+                )
+
+        def stage1_w(k):
+            fh, g = (k // 2) % 2, k % 2
+            w_t[k] = work.tile([P, 4, 512], BF16, name="w_t", align_bytes=64, bufs=3)
+            for t in range(4):
+                ft = 4 * fh + t
+                nc.vector.scalar_tensor_tensor(
+                    out=w_t[k][:, t, :],
+                    in0=accs[k, t][:],
+                    scalar=cs[:, ft : ft + 1],
+                    in1=mu_t[:, ft, 512 * g : 512 * g + 512],
+                    op0=MULT,
+                    op1=ADD,
+                )
+
+        def w_turn(k, copies):
+            w_grp[k] = work.tile([P, 2048], BF16, name="w_grp", align_bytes=64, bufs=3)
+            for pr in range(2):
+                ps = tr_pool.tile([P, 512], F32, name="tr")
+                for l in range(2):
+                    words = w_t[k][:, 2 * pr + l, :].bitcast(F32)
+                    for v in range(2):
+                        c0 = 128 * (2 * l + v)
+                        nc.tensor.transpose(ps[:, c0 : c0 + 128], words[:, 128 * v : 128 * v + 128], ident_f32[:])
+                copies[pr](
+                    out=w_grp[k][:].bitcast(F32)[:, 512 * pr : 512 * pr + 512].rearrange("p (l f v) -> p l f v", l=2, v=2),
+                    in_=ps[:].rearrange("p (l v f) -> p l f v", l=2, v=2),
+                )
+
+        def w_quant(k):
+            w_codes[k] = work.tile([P, 512], U32, name="w_codes", align_bytes=64, bufs=6)
+            w_scales[k] = work.tile([P, 512], U8, name="w_scales", align_bytes=64, bufs=6)
+            nc.vector.quantize_mx(out=w_codes[k][:].bitcast(FP8X4), scales=w_scales[k][:], in_=w_grp[k][:])
+
+        def stage2_mx(h, m):
+            s = h // 2
+            accs["o", h, m] = acc_pool.tile([P, 512], F32, name="acc")
+            for g in range(2):
+                cols = slice(128 * g, 128 * g + 128)
+                nc.tensor.matmul_mx(
+                    out=accs["o", h, m][:],
+                    lhsT=x_codes[s, m][:, cols].bitcast(FP8X4),
+                    lhsT_scale=x_scales[s, m][:, cols],
+                    rhs=w_codes[2 * h + g][:].bitcast(FP8X4),
+                    rhs_scale=w_scales[2 * h + g][:],
+                    start=(g == 0),
+                    stop=(g == 1),
+                )
+
+        def bias_add(h, m):
+            s, fh = h // 2, h % 2
+            cols = slice(512 * fh, 512 * fh + 512)
+            o_f32[h, m] = work.tile([P, 512], F32, name="o_f32", align_bytes=64, bufs=6)
+            nc.vector.tensor_tensor(out=o_f32[h, m][:], in0=accs["o", h, m][:], in1=b_all[:, cols], op=ADD)
+            nc.sync.dma_start(out=out_0[s, 128 * m : 128 * m + 128, cols], in_=o_f32[h, m][:])
+
+        def o_round(h, m, copy):
+            o_bf[h, m] = work.tile([P, 512], BF16, name="o_bf", align_bytes=64, bufs=6)
+            copy(
+                out=o_bf[h, m][:].rearrange("p (v q e) -> p v q e", v=2, e=2),
+                in_=o_f32[h, m][:].rearrange("p (q v e) -> p v q e", v=2, e=2),
+            )
+
+        def o_turn(h, ms, copy):
+            if ms[0] == 0:
+                o_grp[h] = work.tile([P, 1536], BF16, name="o_grp", align_bytes=64, bufs=3)
+            n = len(ms)
+            ps = tr_pool.tile([P, 512], F32, name="tr")
+            for i, m in enumerate(ms):
+                words = o_bf[h, m][:].bitcast(F32)
+                for v in range(2):
+                    c0 = 128 * (2 * i + v)
+                    nc.tensor.transpose(ps[:, c0 : c0 + 128], words[:, 128 * v : 128 * v + 128], ident_f32[:])
+            w0 = 256 * ms[0]
+            copy(
+                out=o_grp[h][:].bitcast(F32)[:, w0 : w0 + 256 * n].rearrange("p (m r v) -> p m r v", m=n, v=2),
+                in_=ps[:, 0 : 256 * n].rearrange("p (m v r) -> p m r v", m=n, v=2),
+            )
+
+        def o_quant(h, ms):
+            s, fh = h // 2, h % 2
+            if ms[0] == 0:
+                o_codes[h] = work.tile([P, B], U32, name="o_codes", align_bytes=64, bufs=3)
+                if fh == 0:
+                    o_scales[s] = work.tile([P, 2, B], U8, name="o_scales", align_bytes=64, bufs=2)
+            lo, hi = 128 * ms[0], 128 * (ms[-1] + 1)
+            nc.vector.quantize_mx(
+                out=o_codes[h][:, lo:hi].bitcast(FP8X4),
+                scales=o_scales[s][:, fh, lo:hi],
+                in_=o_grp[h][:, 4 * lo : 4 * hi],
+            )
+            if ms[-1] == 2:
+                cols = slice(B * s, B * s + B)
+                nc.sync.dma_start(
+                    out=out_1[fh, :, cols, :].rearrange("p m t -> p (m t)").bitcast(I32),
+                    in_=o_codes[h][:].bitcast(I32),
+                )
+                if fh == 1:
+                    for q in range(4):
+                        nc.sync.dma_start(
+                            out=out_2[:, 4 * q : 4 * q + 4, cols].rearrange("g q m -> q g m").bitcast(I32),
+                            in_=o_scales[s][32 * q : 32 * q + 4, :, :].bitcast(I32),
+                        )
+
+        ctx.enter_context(tc.manual_schedule())
+        noise_copy(0, 0, copy_v, 0, 1)
+        noise_quant(0, 0)
+        prep_u(0, (copy_s, copy_v))
+        prep_cs()
+        for ft in range(4):
+            prep_mu(0, ft, (copy_s, copy_v)[ft % 2])
+        last = 4 * S
+        for k in range(last + 6):
+            if k < last:
+                stage1_mx(k)
+            h_even = (k - 4) // 2
+            if k >= 4 and k % 2 == 0 and h_even < 2 * S:
+                stage2_mx(h_even, 0)
+                stage2_mx(h_even, 1)
+            if k >= 5 and k % 2 == 1 and h_even < 2 * S:
+                stage2_mx(h_even, 2)
+            if k < last:
+                stage1_w(k)
+            if 2 <= k < last + 2:
+                w_quant(k - 2)
+            if k == 0:
+                prep_u(1, (copy_s, copy_s))
+                for ft in range(4):
+                    prep_mu(1, ft, copy_s)
+                noise_copy(0, 1, copy_v, 0, 1)
+            if k == 1:
+                noise_quant(0, 1)
+                for ft in range(4, 8):
+                    prep_mu(0, ft, copy_s)
+            if k == 2:
+                for ft in range(4, 8):
+                    prep_mu(1, ft, copy_s)
+            j = (k + 3) // 2
+            if 2 <= j < 2 * S:
+                if (k + 3) % 2 == 0:
+                    noise_copy(j // 2, j % 2, copy_s, 0, 2)
+                else:
+                    noise_copy(j // 2, j % 2, copy_s, 1, 2)
+                    noise_quant(j // 2, j % 2)
+            if k >= 4 and h_even < 2 * S:
+                for m in ((0, 1) if k % 2 == 0 else (2,)):
+                    bias_add(h_even, m)
+                    o_round(h_even, m, copy_s)
+            if 1 <= k < last + 1:
+                w_turn(k - 1, (copy_s, copy_s))
+            h_prev = (k - 5) // 2
+            if k >= 5 and h_prev < 2 * S:
+                ms = (0, 1) if (k - 5) % 2 == 0 else (2,)
+                o_turn(h_prev, ms, copy_s)
+                o_quant(h_prev, ms)
+            sx, mx = k // 4, k % 4 - 1
+            if sx < S and mx >= 0:
+                x_turn(sx, mx, copy_s)
+                x_quant(sx, mx)

@@ -89,6 +89,9 @@ def tile_matrixvariategaussiansampledweights_x1_kernel(tc, x, mu, u, noise, cols
         copy_v = nc.vector.tensor_copy
         copy_s = nc.scalar.copy
 
+        def copy_g(out, in_):
+            nc.gpsimd.tensor_scalar(out=out, in0=in_, scalar1=1.0, scalar2=0.0, op0=MULT, op1=ADD)
+
         def prep_cs():
             ps = tr_pool.tile([P, P], BF16, name="tr")
             nc.tensor.transpose(ps[:], cs_rows[:], ident_bf16[:])
@@ -279,31 +282,42 @@ def tile_matrixvariategaussiansampledweights_x1_kernel(tc, x, mu, u, noise, cols
                         )
 
         ctx.enter_context(tc.manual_schedule())
-        noise_copy(0, 0, copy_v, 0, 1)
-        noise_quant(0, 0)
         prep_u(0, (copy_s, copy_v))
+        noise_copy(0, 0, copy_s, 0, 2)
+        noise_copy(0, 0, copy_v, 1, 2)
+        noise_quant(0, 0)
         prep_cs()
         for ft in range(4):
-            prep_mu(0, ft, (copy_s, copy_v)[ft % 2])
+            prep_mu(0, ft, copy_s)
+        noise_copy(0, 1, copy_g, 0, 2)
+        noise_copy(0, 1, copy_g, 1, 2)
         last = 4 * S
-        for k in range(last + 6):
-            if k < last:
-                stage1_mx(k)
-            h_even = (k - 4) // 2
-            if k >= 4 and k % 2 == 0 and h_even < 2 * S:
-                stage2_mx(h_even, 0)
-                stage2_mx(h_even, 1)
-            if k >= 5 and k % 2 == 1 and h_even < 2 * S:
-                stage2_mx(h_even, 2)
-            if k < last:
-                stage1_w(k)
-            if 2 <= k < last + 2:
+
+        def o_parts(k, lag):
+            h, odd = divmod(k - lag - 3, 2)
+            return (h, (2,) if odd else (0, 1)) if 0 <= h < 2 * S else (None, ())
+
+        for k in range(last):
+            h0, ms0 = o_parts(k, 0)
+            h1, ms1 = o_parts(k, 1)
+            h2, ms2 = o_parts(k, 2)
+            j, second = divmod(k + 3, 2)
+            stage1_mx(k)
+            stage1_w(k)
+            if 2 <= k:
                 w_quant(k - 2)
+            if 2 <= j - 1 < 2 * S and not second:
+                noise_quant((j - 1) // 2, (j - 1) % 2)
+            if ms2:
+                o_quant(h2, ms2)
+            if k >= 1 and (k - 1) % 4 < 3:
+                x_quant((k - 1) // 4, (k - 1) % 4)
+            for m in ms1:
+                o_round(h1, m, copy_s)
             if k == 0:
                 prep_u(1, (copy_s, copy_s))
                 for ft in range(4):
                     prep_mu(1, ft, copy_s)
-                noise_copy(0, 1, copy_v, 0, 1)
             if k == 1:
                 noise_quant(0, 1)
                 for ft in range(4, 8):
@@ -311,25 +325,40 @@ def tile_matrixvariategaussiansampledweights_x1_kernel(tc, x, mu, u, noise, cols
             if k == 2:
                 for ft in range(4, 8):
                     prep_mu(1, ft, copy_s)
-            j = (k + 3) // 2
-            if 2 <= j < 2 * S:
-                if (k + 3) % 2 == 0:
-                    noise_copy(j // 2, j % 2, copy_s, 0, 2)
-                else:
-                    noise_copy(j // 2, j % 2, copy_s, 1, 2)
-                    noise_quant(j // 2, j % 2)
-            if k >= 4 and h_even < 2 * S:
-                for m in ((0, 1) if k % 2 == 0 else (2,)):
-                    bias_add(h_even, m)
-                    o_round(h_even, m, copy_s)
-            if 1 <= k < last + 1:
+            if 1 <= k:
                 w_turn(k - 1, (copy_s, copy_s))
-            h_prev = (k - 5) // 2
-            if k >= 5 and h_prev < 2 * S:
-                ms = (0, 1) if (k - 5) % 2 == 0 else (2,)
-                o_turn(h_prev, ms, copy_s)
-                o_quant(h_prev, ms)
-            sx, mx = k // 4, k % 4 - 1
-            if sx < S and mx >= 0:
-                x_turn(sx, mx, copy_s)
-                x_quant(sx, mx)
+            if 2 <= j < 2 * S:
+                noise_copy(j // 2, j % 2, copy_s, second, 2)
+            if ms1:
+                o_turn(h1, ms1, copy_s)
+            if k % 4 < 3:
+                x_turn(k // 4, k % 4, copy_s)
+            for m in ms0:
+                stage2_mx(h0, m)
+            for m in ms0:
+                bias_add(h0, m)
+        w_turn(last - 1, (copy_s, copy_v))
+        w_quant(last - 2)
+        w_quant(last - 1)
+        stage2_mx(6, 2)
+        for m in range(3):
+            stage2_mx(7, m)
+        o_quant(5, (2,))
+        o_round(6, 0, copy_s)
+        o_round(6, 1, copy_s)
+        bias_add(6, 2)
+        o_turn(6, (0, 1), copy_s)
+        o_round(6, 2, copy_s)
+        bias_add(7, 0)
+        bias_add(7, 1)
+        o_quant(6, (0, 1))
+        o_round(7, 0, copy_s)
+        bias_add(7, 2)
+        o_round(7, 1, copy_s)
+        o_turn(6, (2,), copy_v)
+        o_turn(7, (0, 1), copy_s)
+        o_round(7, 2, copy_v)
+        o_quant(6, (2,))
+        o_turn(7, (2,), copy_v)
+        o_quant(7, (0, 1))
+        o_quant(7, (2,))

@@ -46,8 +46,10 @@ def tile_matrixvariategaussiansampledweights_x1_kernel(tc, x, mu, u, noise, cols
             cols = slice(512 * fh, 512 * fh + 512)
             nc.sync.dma_start(out=n_raw[s][:, :, cols], in_=noise[s, :, cols].rearrange("(p j) f -> p j f", j=4))
 
-        def load_u(g):
-            nc.sync.dma_start(out=u_raw[g][:], in_=u[512 * g : 512 * g + 512, :].rearrange("(q j) r -> q j r", j=4))
+        def load_u(g, u2s=range(2)):
+            for u2 in u2s:
+                rows = u[512 * g : 512 * g + 512, :].rearrange("(q j) r -> q j r", j=4)
+                nc.sync.dma_start(out=u_raw[g][:, 2 * u2 : 2 * u2 + 2, :], in_=rows[:, 2 * u2 : 2 * u2 + 2, :])
 
         def load_mu(g, fh):
             cols = slice(512 * fh, 512 * fh + 512)
@@ -63,13 +65,17 @@ def tile_matrixvariategaussiansampledweights_x1_kernel(tc, x, mu, u, noise, cols
         load_u(1)
         load_mu(1, 0)
         load_x(0)
-        load_noise_half(0, 1)
-        load_mu(0, 1)
-        load_mu(1, 1)
+        load_noise_half(1, 0)
         nc.sync.dma_start(out=b_all[:], in_=b.partition_broadcast(P))
-        for s in range(1, S):
-            nc.sync.dma_start(out=n_raw[s][:], in_=noise[s].rearrange("(p j) f -> p j f", j=4))
-            load_x(s)
+        load_mu(0, 1)
+        load_x(1)
+        load_noise_half(2, 0)
+        load_mu(1, 1)
+        load_x(2)
+        load_noise_half(3, 0)
+        load_x(3)
+        for s in range(S):
+            load_noise_half(s, 1)
 
         ident_f32 = const.tile([P, P], F32, name="ident_f32", align_bytes=64)
         make_identity(nc, ident_f32[:])
@@ -150,22 +156,22 @@ def tile_matrixvariategaussiansampledweights_x1_kernel(tc, x, mu, u, noise, cols
                 for v in range(2):
                     c0 = 128 * (2 * g + v)
                     nc.tensor.transpose(ps[:, c0 : c0 + 128], words[:, 256 * g + v : 256 * g + 256 : 2], ident_f32[:])
-            x_grp[s, m] = work.tile([P, 1024], BF16, name="x_grp", align_bytes=64, bufs=4)
+            x_grp[s, m] = work.tile([P, 1024], BF16, name="x_grp", align_bytes=64, bufs=5)
             copy(
                 out=x_grp[s, m][:].bitcast(F32).rearrange("p (g r v) -> p g r v", g=2, v=2),
                 in_=ps[:].rearrange("p (g v r) -> p g r v", g=2, v=2),
             )
 
         def x_quant(s, m):
-            x_codes[s, m] = work.tile([P, 256], U32, name="x_codes", align_bytes=64, bufs=7)
-            x_scales[s, m] = work.tile([P, 256], U8, name="x_scales", align_bytes=64, bufs=7)
+            x_codes[s, m] = work.tile([P, 256], U32, name="x_codes", align_bytes=64, bufs=12)
+            x_scales[s, m] = work.tile([P, 256], U8, name="x_scales", align_bytes=64, bufs=12)
             nc.vector.quantize_mx(out=x_codes[s, m][:].bitcast(FP8X4), scales=x_scales[s, m][:], in_=x_grp[s, m][:])
 
         accs = {}
 
-        def stage1_mx(k):
-            s, fh, g = k // 4, (k // 2) % 2, k % 2
-            for t in range(4):
+        def stage1_mx(k, ts=range(4)):
+            s, fh, g = (k // 2) % 4, k // 8, k % 2
+            for t in ts:
                 accs[k, t] = acc_pool.tile([P, 512], F32, name="acc")
                 cols = slice(128 * t, 128 * t + 128)
                 nc.tensor.matmul_mx(
@@ -178,10 +184,11 @@ def tile_matrixvariategaussiansampledweights_x1_kernel(tc, x, mu, u, noise, cols
                     stop=True,
                 )
 
-        def stage1_w(k):
-            fh, g = (k // 2) % 2, k % 2
-            w_t[k] = work.tile([P, 4, 512], BF16, name="w_t", align_bytes=64, bufs=3)
-            for t in range(4):
+        def stage1_w(k, ts=range(4)):
+            fh, g = k // 8, k % 2
+            if 0 in ts:
+                w_t[k] = work.tile([P, 4, 512], BF16, name="w_t", align_bytes=64, bufs=3)
+            for t in ts:
                 ft = 4 * fh + t
                 nc.vector.scalar_tensor_tensor(
                     out=w_t[k][:, t, :],
@@ -192,9 +199,10 @@ def tile_matrixvariategaussiansampledweights_x1_kernel(tc, x, mu, u, noise, cols
                     op1=ADD,
                 )
 
-        def w_turn(k, copies):
-            w_grp[k] = work.tile([P, 2048], BF16, name="w_grp", align_bytes=64, bufs=3)
-            for pr in range(2):
+        def w_turn(k, copies, prs=(0, 1)):
+            if 0 in prs:
+                w_grp[k] = work.tile([P, 2048], BF16, name="w_grp", align_bytes=64, bufs=3)
+            for pr in prs:
                 ps = tr_pool.tile([P, 512], F32, name="tr")
                 for l in range(2):
                     words = w_t[k][:, 2 * pr + l, :].bitcast(F32)
@@ -212,7 +220,7 @@ def tile_matrixvariategaussiansampledweights_x1_kernel(tc, x, mu, u, noise, cols
             nc.vector.quantize_mx(out=w_codes[k][:].bitcast(FP8X4), scales=w_scales[k][:], in_=w_grp[k][:])
 
         def stage2_mx(h, m):
-            s = h // 2
+            s = h % 4
             accs["o", h, m] = acc_pool.tile([P, 512], F32, name="acc")
             for g in range(2):
                 cols = slice(128 * g, 128 * g + 128)
@@ -227,10 +235,15 @@ def tile_matrixvariategaussiansampledweights_x1_kernel(tc, x, mu, u, noise, cols
                 )
 
         def bias_add(h, m):
-            s, fh = h // 2, h % 2
+            s, fh = h % 4, h // 4
             cols = slice(512 * fh, 512 * fh + 512)
             o_f32[h, m] = work.tile([P, 512], F32, name="o_f32", align_bytes=64, bufs=6)
-            nc.vector.tensor_tensor(out=o_f32[h, m][:], in0=accs["o", h, m][:], in1=b_all[:, cols], op=ADD)
+            if m in ():
+                o_raw = work.tile([P, 512], F32, name="o_raw", align_bytes=64, bufs=2)
+                copy_s(out=o_raw[:], in_=accs["o", h, m][:])
+                nc.gpsimd.tensor_tensor(out=o_f32[h, m][:], in0=o_raw[:], in1=b_all[:, cols], op=ADD)
+            else:
+                nc.vector.tensor_tensor(out=o_f32[h, m][:], in0=accs["o", h, m][:], in1=b_all[:, cols], op=ADD)
             nc.sync.dma_start(out=out_0[s, 128 * m : 128 * m + 128, cols], in_=o_f32[h, m][:])
 
         def o_round(h, m, copy):
@@ -257,15 +270,15 @@ def tile_matrixvariategaussiansampledweights_x1_kernel(tc, x, mu, u, noise, cols
             )
 
         def o_quant(h, ms):
-            s, fh = h // 2, h % 2
+            s, fh = h % 4, h // 4
             if ms[0] == 0:
                 o_codes[h] = work.tile([P, B], U32, name="o_codes", align_bytes=64, bufs=3)
-                if fh == 0:
-                    o_scales[s] = work.tile([P, 2, B], U8, name="o_scales", align_bytes=64, bufs=2)
+                if s == 0:
+                    o_scales[fh] = work.tile([P, S * B], U8, name="o_scales", align_bytes=64, bufs=2)
             lo, hi = 128 * ms[0], 128 * (ms[-1] + 1)
             nc.vector.quantize_mx(
                 out=o_codes[h][:, lo:hi].bitcast(FP8X4),
-                scales=o_scales[s][:, fh, lo:hi],
+                scales=o_scales[fh][:, B * s + lo : B * s + hi],
                 in_=o_grp[h][:, 4 * lo : 4 * hi],
             )
             if ms[-1] == 2:
@@ -274,11 +287,11 @@ def tile_matrixvariategaussiansampledweights_x1_kernel(tc, x, mu, u, noise, cols
                     out=out_1[fh, :, cols, :].rearrange("p m t -> p (m t)").bitcast(I32),
                     in_=o_codes[h][:].bitcast(I32),
                 )
-                if fh == 1:
+                if s == S - 1:
                     for q in range(4):
                         nc.sync.dma_start(
-                            out=out_2[:, 4 * q : 4 * q + 4, cols].rearrange("g q m -> q g m").bitcast(I32),
-                            in_=o_scales[s][32 * q : 32 * q + 4, :, :].bitcast(I32),
+                            out=out_2[fh, 4 * q : 4 * q + 4, :].bitcast(I32),
+                            in_=o_scales[fh][32 * q : 32 * q + 4, :].bitcast(I32),
                         )
 
         ctx.enter_context(tc.manual_schedule())
@@ -289,54 +302,71 @@ def tile_matrixvariategaussiansampledweights_x1_kernel(tc, x, mu, u, noise, cols
         prep_cs()
         for ft in range(4):
             prep_mu(0, ft, copy_s)
-        noise_copy(0, 1, copy_g, 0, 2)
-        noise_copy(0, 1, copy_g, 1, 2)
         last = 4 * S
 
         def o_parts(k, lag):
             h, odd = divmod(k - lag - 3, 2)
             return (h, (2,) if odd else (0, 1)) if 0 <= h < 2 * S else (None, ())
 
-        for k in range(last):
+        def x_parts(k):
+            s, odd = divmod(k, 2)
+            return ((s, 2),) if odd and 0 <= s < S else ((s, 0), (s, 1)) if 0 <= s < S else ()
+
+        def step(k, seq):
             h0, ms0 = o_parts(k, 0)
             h1, ms1 = o_parts(k, 1)
             h2, ms2 = o_parts(k, 2)
             j, second = divmod(k + 3, 2)
-            stage1_mx(k)
-            stage1_w(k)
-            if 2 <= k:
-                w_quant(k - 2)
-            if 2 <= j - 1 < 2 * S and not second:
-                noise_quant((j - 1) // 2, (j - 1) % 2)
-            if ms2:
-                o_quant(h2, ms2)
-            if k >= 1 and (k - 1) % 4 < 3:
-                x_quant((k - 1) // 4, (k - 1) % 4)
-            for m in ms1:
-                o_round(h1, m, copy_s)
-            if k == 0:
-                prep_u(1, (copy_s, copy_s))
-                for ft in range(4):
-                    prep_mu(1, ft, copy_s)
-            if k == 1:
-                noise_quant(0, 1)
-                for ft in range(4, 8):
-                    prep_mu(0, ft, copy_s)
-            if k == 2:
-                for ft in range(4, 8):
-                    prep_mu(1, ft, copy_s)
-            if 1 <= k:
-                w_turn(k - 1, (copy_s, copy_s))
-            if 2 <= j < 2 * S:
-                noise_copy(j // 2, j % 2, copy_s, second, 2)
-            if ms1:
-                o_turn(h1, ms1, copy_s)
-            if k % 4 < 3:
-                x_turn(k // 4, k % 4, copy_s)
-            for m in ms0:
-                stage2_mx(h0, m)
-            for m in ms0:
-                bias_add(h0, m)
+            for a in seq:
+                if a == "a":
+                    stage1_mx(k, (0, 1))
+                if a == "b":
+                    stage1_mx(k, (2, 3))
+                if a == "s":
+                    stage1_w(k, (0, 1))
+                if a == "z":
+                    stage1_w(k, (2, 3))
+                if a == "q" and 2 <= k:
+                    w_quant(k - 2)
+                if a == "n" and 1 <= j - 1 < 2 * S and not second:
+                    noise_quant((j - 1) % 4, (j - 1) // 4)
+                if a == "o" and ms2:
+                    o_quant(h2, ms2)
+                if a == "x":
+                    for i in x_parts(k - 1):
+                        x_quant(*i)
+                if a == "R":
+                    for m in ms1:
+                        o_round(h1, m, copy_s)
+                if a == "H":
+                    if k == 0:
+                        prep_u(1, (copy_s, copy_s))
+                        for ft in range(4):
+                            prep_mu(1, ft, copy_s)
+                    if 3 <= k < 7:
+                        for i in (2 * k - 6, 2 * k - 5):
+                            prep_mu(i // 4, 4 + i % 4, copy_s)
+                if a == "T" and 1 <= k:
+                    w_turn(k - 1, (copy_s, copy_s), (0,))
+                if a == "t" and 1 <= k:
+                    w_turn(k - 1, (copy_s, copy_s), (1,))
+                if a == "N" and 1 <= j < 2 * S:
+                    for part in ((0, 1) if k == 0 else (second,)):
+                        noise_copy(j % 4, j // 4, copy_s, part, 2)
+                if a == "U" and ms1:
+                    o_turn(h1, ms1, copy_s)
+                if a == "X":
+                    for i in x_parts(k):
+                        x_turn(*i, copy_s)
+                if a == "M":
+                    for m in ms0:
+                        stage2_mx(h0, m)
+                if a == "B":
+                    for m in ms0:
+                        bias_add(h0, m)
+
+        for k in range(last):
+            step(k, "axHMobNTRXnBsUqtz" if k == 0 else "HaRTnxtNqXbMsoUzB" if k == 1 else "RoaTnqbUsHNzMBtXx")
         w_turn(last - 1, (copy_s, copy_v))
         w_quant(last - 2)
         w_quant(last - 1)

from contextlib import ExitStack

import concourse.mybir as mybir
from concourse.masks import make_identity

F32 = mybir.dt.float32
BF16 = mybir.dt.bfloat16
I32 = mybir.dt.int32
U32 = mybir.dt.uint32
U8 = mybir.dt.uint8
FP8X4 = mybir.dt.float8_e4m3fn_x4
MULT = mybir.AluOpType.mult
ADD = mybir.AluOpType.add

S, B, D, R, F = 4, 384, 1024, 512, 1024
FLOPS = 2 * S * D * R * F + 2 * S * B * D * F
P = 128


def tile_matrixvariategaussiansampledweights_x1_kernel(tc, x, mu, u, noise, colscale, b, out_0, out_1, out_2):
    nc = tc.nc
    with ExitStack() as ctx:
        const = ctx.enter_context(tc.tile_pool(name="const", bufs=1))
        raw = ctx.enter_context(tc.tile_pool(name="raw", bufs=1))
        work = ctx.enter_context(tc.tile_pool(name="work", bufs=3))
        acc_pool = ctx.enter_context(tc.psum_pool(name="acc_pool", bufs=5))
        tr_pool = ctx.enter_context(tc.psum_pool(name="tr_pool", bufs=3))

        n_raw = {}
        for s in range(S):
            n_raw[s] = raw.tile([P, 4, F], BF16, name="n_raw%d" % s, align_bytes=64)
        u_raw = {}
        mu_raw = {}
        for g in range(2):
            u_raw[g] = raw.tile([P, 4, R], BF16, name="u_raw%d" % g, align_bytes=64)
            for fh in range(2):
                mu_raw[g, fh] = raw.tile([P, 4, 512], BF16, name="mu_raw%d%d" % (g, fh), align_bytes=64)
        x_raw = {}
        for s in range(S):
            x_raw[s] = raw.tile([P, 3, D], BF16, name="x_raw%d" % s, align_bytes=64)
        cs_rows = const.tile([P, P], BF16, name="cs_rows", align_bytes=64)
        b_all = const.tile([P, F], BF16, name="b_all", align_bytes=64)
        nc.vector.memset(cs_rows[:], 0.0)

        def load_noise_half(s, fh):
            cols = slice(512 * fh, 512 * fh + 512)
            nc.sync.dma_start(out=n_raw[s][:, :, cols], in_=noise[s, :, cols].rearrange("(p j) f -> p j f", j=4))

        def load_u(g, u2s=range(2)):
            for u2 in u2s:
                rows = u[512 * g : 512 * g + 512, :].rearrange("(q j) r -> q j r", j=4)
                nc.sync.dma_start(out=u_raw[g][:, 2 * u2 : 2 * u2 + 2, :], in_=rows[:, 2 * u2 : 2 * u2 + 2, :])

        def load_mu(g, fh):
            cols = slice(512 * fh, 512 * fh + 512)
            nc.sync.dma_start(out=mu_raw[g, fh][:], in_=mu[512 * g : 512 * g + 512, cols].rearrange("(q j) f -> q j f", j=4))

        def load_x(s):
            nc.sync.dma_start(out=x_raw[s][:], in_=x[s].rearrange("(m p) d -> p m d", p=P))

        load_u(0)
        load_noise_half(0, 0)
        nc.sync.dma_start(out=cs_rows[0:8, :], in_=colscale.rearrange("(c p) -> c p", p=P))
        load_mu(0, 0)
        load_u(1)
        load_mu(1, 0)
        load_x(0)
        load_noise_half(1, 0)
        nc.sync.dma_start(out=b_all[:], in_=b.partition_broadcast(P))
        load_mu(0, 1)
        load_x(1)
        load_noise_half(2, 0)
        load_mu(1, 1)
        load_x(2)
        load_noise_half(3, 0)
        load_x(3)
        for s in range(S):
            load_noise_half(s, 1)

        ident_f32 = const.tile([P, P], F32, name="ident_f32", align_bytes=64)
        make_identity(nc, ident_f32[:])
        ident_bf16 = const.tile([P, P], BF16, name="ident_bf16", align_bytes=64)
        make_identity(nc, ident_bf16[:])

        cs = const.tile([P, 8], F32, name="cs")
        mu_t = const.tile([P, 8, D], BF16, name="mu_t", align_bytes=64)
        u_codes, u_scales = {}, {}
        n_codes, n_scales = {}, {}
        x_codes, x_scales = {}, {}
        w_codes, w_scales = {}, {}
        w_t, w_grp = {}, {}
        n_grp, x_grp = {}, {}
        o_f32, o_bf, o_grp = {}, {}, {}
        o_codes, o_scales = {}, {}
        copy_v = nc.vector.tensor_copy
        copy_s = nc.scalar.copy

        def copy_g(out, in_):
            nc.gpsimd.tensor_scalar(out=out, in0=in_, scalar1=1.0, scalar2=0.0, op0=MULT, op1=ADD)

        def prep_cs():
            ps = tr_pool.tile([P, P], BF16, name="tr")
            nc.tensor.transpose(ps[:], cs_rows[:], ident_bf16[:])
            copy_v(out=cs[:], in_=ps[:, 0:8])

        def prep_u(g, copies):
            grp = work.tile([P, 2048], BF16, name="u_grp", align_bytes=64, bufs=2)
            for u2 in range(2):
                ps = tr_pool.tile([P, 512], F32, name="tr")
                for e in range(2):
                    words = u_raw[g][:, 2 * u2 + e, :].bitcast(F32)
                    for h in range(2):
                        c0 = 128 * (2 * e + h)
                        nc.tensor.transpose(ps[:, c0 : c0 + 128], words[:, h : 256 : 2], ident_f32[:])
                copies[u2](
                    out=grp[:].bitcast(F32)[:, 512 * u2 : 512 * u2 + 512].rearrange("p (q e h) -> p q e h", e=2, h=2),
                    in_=ps[:].rearrange("p (e h q) -> p q e h", e=2, h=2),
                )
            u_codes[g] = const.tile([P, 512], U32, name="u_codes%d" % g, align_bytes=64)
            u_scales[g] = const.tile([P, 512], U8, name="u_scales%d" % g, align_bytes=64)
            nc.vector.quantize_mx(out=u_codes[g][:].bitcast(FP8X4), scales=u_scales[g][:], in_=grp[:])

        def prep_mu(g, ft, copy):
            ps = tr_pool.tile([P, 512], BF16, name="tr")
            c0 = 128 * (ft % 4)
            for j in range(4):
                nc.tensor.transpose(ps[:, 128 * j : 128 * j + 128], mu_raw[g, ft // 4][:, j, c0 : c0 + 128], ident_bf16[:])
            copy(
                out=mu_t[:, ft, 512 * g : 512 * g + 512].rearrange("p (v q e) -> p v q e", v=2, e=2),
                in_=ps[:].rearrange("p (v e q) -> p v q e", v=2, e=2),
            )

        def noise_copy(s, fh, copy, part, parts):
            if part == 0:
                n_grp[s, fh] = work.tile([P, 512, 4], BF16, name="n_grp", align_bytes=64, bufs=3)
            w = 512 // parts
            lo = w * part
            copy(
                out=n_grp[s, fh][:, lo : lo + w, :],
                in_=n_raw[s][:, :, 512 * fh + lo : 512 * fh + lo + w].rearrange("p j f -> p f j"),
            )

        def noise_quant(s, fh):
            n_codes[s, fh] = work.tile([P, 512], U32, name="n_codes", align_bytes=64, bufs=4)
            n_scales[s, fh] = work.tile([P, 512], U8, name="n_scales", align_bytes=64, bufs=4)
            nc.vector.quantize_mx(
                out=n_codes[s, fh][:].bitcast(FP8X4),
                scales=n_scales[s, fh][:],
                in_=n_grp[s, fh][:].rearrange("p f j -> p (f j)"),
            )

        def x_turn(s, m, copy):
            ps = tr_pool.tile([P, 512], F32, name="tr")
            words = x_raw[s][:, m, :].bitcast(F32)
            for g in range(2):
                for v in range(2):
                    c0 = 128 * (2 * g + v)
                    nc.tensor.transpose(ps[:, c0 : c0 + 128], words[:, 256 * g + v : 256 * g + 256 : 2], ident_f32[:])
            x_grp[s, m] = work.tile([P, 1024], BF16, name="x_grp", align_bytes=64, bufs=5)
            copy(
                out=x_grp[s, m][:].bitcast(F32).rearrange("p (g r v) -> p g r v", g=2, v=2),
                in_=ps[:].rearrange("p (g v r) -> p g r v", g=2, v=2),
            )

        def x_quant(s, m):
            x_codes[s, m] = work.tile([P, 256], U32, name="x_codes", align_bytes=64, bufs=12)
            x_scales[s, m] = work.tile([P, 256], U8, name="x_scales", align_bytes=64, bufs=12)
            nc.vector.quantize_mx(out=x_codes[s, m][:].bitcast(FP8X4), scales=x_scales[s, m][:], in_=x_grp[s, m][:])

        accs = {}

        def stage1_mx(k, ts=range(4)):
            s, fh, g = (k // 2) % 4, k // 8, k % 2
            for t in ts:
                accs[k, t] = acc_pool.tile([P, 512], F32, name="acc")
                cols = slice(128 * t, 128 * t + 128)
                nc.tensor.matmul_mx(
                    out=accs[k, t][:],
                    lhsT=n_codes[s, fh][:, cols].bitcast(FP8X4),
                    lhsT_scale=n_scales[s, fh][:, cols],
                    rhs=u_codes[g][:].bitcast(FP8X4),
                    rhs_scale=u_scales[g][:],
                    start=True,
                    stop=True,
                )

        def stage1_w(k, ts=range(4)):
            fh, g = k // 8, k % 2
            if 0 in ts:
                w_t[k] = work.tile([P, 4, 512], BF16, name="w_t", align_bytes=64, bufs=3)
            for t in ts:
                ft = 4 * fh + t
                nc.vector.scalar_tensor_tensor(
                    out=w_t[k][:, t, :],
                    in0=accs[k, t][:],
                    scalar=cs[:, ft : ft + 1],
                    in1=mu_t[:, ft, 512 * g : 512 * g + 512],
                    op0=MULT,
                    op1=ADD,
                )

        def w_turn(k, copies, prs=(0, 1)):
            if 0 in prs:
                w_grp[k] = work.tile([P, 2048], BF16, name="w_grp", align_bytes=64, bufs=3)
            for pr in prs:
                ps = tr_pool.tile([P, 512], F32, name="tr")
                for l in range(2):
                    words = w_t[k][:, 2 * pr + l, :].bitcast(F32)
                    for v in range(2):
                        c0 = 128 * (2 * l + v)
                        nc.tensor.transpose(ps[:, c0 : c0 + 128], words[:, 128 * v : 128 * v + 128], ident_f32[:])
                copies[pr](
                    out=w_grp[k][:].bitcast(F32)[:, 512 * pr : 512 * pr + 512].rearrange("p (l f v) -> p l f v", l=2, v=2),
                    in_=ps[:].rearrange("p (l v f) -> p l f v", l=2, v=2),
                )

        def w_quant(k):
            w_codes[k] = work.tile([P, 512], U32, name="w_codes", align_bytes=64, bufs=6)
            w_scales[k] = work.tile([P, 512], U8, name="w_scales", align_bytes=64, bufs=6)
            nc.vector.quantize_mx(out=w_codes[k][:].bitcast(FP8X4), scales=w_scales[k][:], in_=w_grp[k][:])

        def stage2_mx(h, m):
            s = h % 4
            accs["o", h, m] = acc_pool.tile([P, 512], F32, name="acc")
            for g in range(2):
                cols = slice(128 * g, 128 * g + 128)
                nc.tensor.matmul_mx(
                    out=accs["o", h, m][:],
                    lhsT=x_codes[s, m][:, cols].bitcast(FP8X4),
                    lhsT_scale=x_scales[s, m][:, cols],
                    rhs=w_codes[2 * h + g][:].bitcast(FP8X4),
                    rhs_scale=w_scales[2 * h + g][:],
                    start=(g == 0),
                    stop=(g == 1),
                )

        def bias_add(h, m):
            s, fh = h % 4, h // 4
            cols = slice(512 * fh, 512 * fh + 512)
            o_f32[h, m] = work.tile([P, 512], F32, name="o_f32", align_bytes=64, bufs=6)
            if m in ():
                o_raw = work.tile([P, 512], F32, name="o_raw", align_bytes=64, bufs=2)
                copy_s(out=o_raw[:], in_=accs["o", h, m][:])
                nc.gpsimd.tensor_tensor(out=o_f32[h, m][:], in0=o_raw[:], in1=b_all[:, cols], op=ADD)
            else:
                nc.vector.tensor_tensor(out=o_f32[h, m][:], in0=accs["o", h, m][:], in1=b_all[:, cols], op=ADD)
            nc.sync.dma_start(out=out_0[s, 128 * m : 128 * m + 128, cols], in_=o_f32[h, m][:])

        def o_round(h, m, copy):
            o_bf[h, m] = work.tile([P, 512], BF16, name="o_bf", align_bytes=64, bufs=6)
            copy(
                out=o_bf[h, m][:].rearrange("p (v q e) -> p v q e", v=2, e=2),
                in_=o_f32[h, m][:].rearrange("p (q v e) -> p v q e", v=2, e=2),
            )

        def o_turn(h, ms, copy):
            if ms[0] == 0:
                o_grp[h] = work.tile([P, 1536], BF16, name="o_grp", align_bytes=64, bufs=3)
            n = len(ms)
            ps = tr_pool.tile([P, 512], F32, name="tr")
            for i, m in enumerate(ms):
                words = o_bf[h, m][:].bitcast(F32)
                for v in range(2):
                    c0 = 128 * (2 * i + v)
                    nc.tensor.transpose(ps[:, c0 : c0 + 128], words[:, 128 * v : 128 * v + 128], ident_f32[:])
            w0 = 256 * ms[0]
            copy(
                out=o_grp[h][:].bitcast(F32)[:, w0 : w0 + 256 * n].rearrange("p (m r v) -> p m r v", m=n, v=2),
                in_=ps[:, 0 : 256 * n].rearrange("p (m v r) -> p m r v", m=n, v=2),
            )

        def o_quant(h, ms):
            s, fh = h % 4, h // 4
            if ms[0] == 0:
                o_codes[h] = work.tile([P, B], U32, name="o_codes", align_bytes=64, bufs=3)
                if s == 0:
                    o_scales[fh] = work.tile([P, S * B], U8, name="o_scales", align_bytes=64, bufs=2)
            lo, hi = 128 * ms[0], 128 * (ms[-1] + 1)
            nc.vector.quantize_mx(
                out=o_codes[h][:, lo:hi].bitcast(FP8X4),
                scales=o_scales[fh][:, B * s + lo : B * s + hi],
                in_=o_grp[h][:, 4 * lo : 4 * hi],
            )
            if ms[-1] == 2:
                cols = slice(B * s, B * s + B)
                nc.sync.dma_start(
                    out=out_1[fh, :, cols, :].rearrange("p m t -> p (m t)").bitcast(I32),
                    in_=o_codes[h][:].bitcast(I32),
                )
                if s == S - 1:
                    for q in range(4):
                        nc.sync.dma_start(
                            out=out_2[fh, 4 * q : 4 * q + 4, :].bitcast(I32),
                            in_=o_scales[fh][32 * q : 32 * q + 4, :].bitcast(I32),
                        )

        ctx.enter_context(tc.manual_schedule())
        prep_u(0, (copy_s, copy_v))
        noise_copy(0, 0, copy_s, 0, 2)
        noise_copy(0, 0, copy_v, 1, 2)
        noise_quant(0, 0)
        prep_cs()
        for ft in range(4):
            prep_mu(0, ft, copy_s)
        last = 4 * S

        def o_parts(k, lag):
            h, odd = divmod(k - lag - 3, 2)
            return (h, (2,) if odd else (0, 1)) if 0 <= h < 2 * S else (None, ())

        def x_parts(k):
            s, odd = divmod(k, 2)
            return ((s, 2),) if odd and 0 <= s < S else ((s, 0), (s, 1)) if 0 <= s < S else ()

        def step(k, seq):
            h0, ms0 = o_parts(k, 0)
            h1, ms1 = o_parts(k, 1)
            h2, ms2 = o_parts(k, 2)
            j, second = divmod(k + 3, 2)
            for a in seq:
                if a == "a":
                    stage1_mx(k, (0, 1))
                if a == "b":
                    stage1_mx(k, (2, 3))
                if a == "s":
                    stage1_w(k, (0, 1))
                if a == "z":
                    stage1_w(k, (2, 3))
                if a == "q" and 2 <= k:
                    w_quant(k - 2)
                if a == "n" and 1 <= j - 1 < 2 * S and not second:
                    noise_quant((j - 1) % 4, (j - 1) // 4)
                if a == "o" and ms2:
                    o_quant(h2, ms2)
                if a == "x":
                    for i in x_parts(k - 1):
                        x_quant(*i)
                if a == "R":
                    for m in ms1:
                        o_round(h1, m, copy_s)
                if a == "H":
                    if k == 0:
                        prep_u(1, (copy_s, copy_s))
                        for ft in range(4):
                            prep_mu(1, ft, copy_s)
                    if 3 <= k < 7:
                        for i in (2 * k - 6, 2 * k - 5):
                            prep_mu(i // 4, 4 + i % 4, copy_s)
                if a == "T" and 1 <= k:
                    w_turn(k - 1, (copy_s, copy_s), (0,))
                if a == "t" and 1 <= k:
                    w_turn(k - 1, (copy_s, copy_s), (1,))
                if a == "N" and 1 <= j < 2 * S:
                    for part in ((0, 1) if k == 0 else (second,)):
                        noise_copy(j % 4, j // 4, copy_s, part, 2)
                if a == "U" and ms1:
                    o_turn(h1, ms1, copy_s)
                if a == "X":
                    for i in x_parts(k):
                        x_turn(*i, copy_s)
                if a == "M":
                    for m in ms0:
                        stage2_mx(h0, m)
                if a == "B":
                    for m in ms0:
                        bias_add(h0, m)

        for k in range(last):
            step(k, "axHMobNTRXnBsUqtz" if k == 0 else "HaRTnxtNqXbMsoUzB" if k == 1 else "RoaTnqbUsHNzMBtXx")
        w_turn(last - 1, (copy_s, copy_v))
        w_quant(last - 2)
        w_quant(last - 1)
        stage2_mx(6, 2)
        for m in range(3):
            stage2_mx(7, m)
        o_quant(5, (2,))
        o_round(6, 0, copy_s)
        o_round(6, 1, copy_s)
        bias_add(6, 2)
        o_turn(6, (0, 1), copy_s)
        o_round(6, 2, copy_s)
        bias_add(7, 0)
        bias_add(7, 1)
        o_quant(6, (0, 1))
        o_round(7, 0, copy_s)
        bias_add(7, 2)
        o_round(7, 1, copy_s)
        o_turn(6, (2,), copy_v)
        o_turn(7, (0, 1), copy_s)
        o_round(7, 2, copy_v)
        o_quant(6, (2,))
        o_turn(7, (2,), copy_v)
        o_quant(7, (0, 1))
        o_quant(7, (2,))
